import numpy as np
import ml_dtypes


def mxq(x, axis, fmt="e4m3"):
    dtype, down = {"e4m3": (ml_dtypes.float8_e4m3fn, 7), "e5m2": (ml_dtypes.float8_e5m2, 14)}[fmt]
    v = np.moveaxis(np.asarray(x, np.float32).astype(ml_dtypes.bfloat16).astype(np.float64), axis, -1)
    blocks = v.reshape(v.shape[:-1] + (-1, 32))
    amax = np.abs(blocks).max(-1, keepdims=True)
    byte = np.maximum(np.where(amax > 0, np.frexp(amax)[1] - 1 + 127, 0) - down, 1)
    scale = np.exp2(byte - 127.0)
    codes = (blocks / scale).astype(np.float32).astype(dtype).astype(np.float64)
    return np.moveaxis((codes * scale).reshape(v.shape), -1, axis)


WIDE = False


def mx_kscale(k):
    if not WIDE:
        return np.ones(k)
    levels = np.array([10, -10, 5, -5, 0])
    if k % 512:
        return np.exp2(np.random.permutation(np.resize(levels, k // 32))).repeat(32)
    a = np.empty((k // 512, 16))
    for p in range(k // 512):
        a[p, :8] = np.random.permutation(np.resize(levels, 8))
        for g in range(8):
            far = levels[np.abs(levels - a[p, g]) >= 10]
            a[p, g + 8] = far[np.random.randint(len(far))]
    return np.exp2(a.ravel()).repeat(32)


def f64(x):
    return np.asarray(x).astype(np.float64)


def striped(idx):
    return np.tile(idx.reshape(-1, 16).T, (8, 1)).astype(np.uint16)


def unstriped(offs):
    return offs[:16].T.reshape(-1).astype(np.int64)


def pack_weight(w):
    k, n = w.shape
    w = f64(np.asarray(w, np.float32).astype(ml_dtypes.bfloat16)).reshape(k // 32, 32, n)
    amax = np.abs(w).max(1)
    byte = np.clip(np.where(amax > 0, np.frexp(amax)[1] - 1 + 127 - 7, 1), 1, 254)
    scaled = (w * np.exp2(127.0 - byte)[:, None, :]).reshape(k, n).astype(np.float32)
    words = np.ascontiguousarray(scaled.reshape(k // 512, 128, 4, n).transpose(0, 1, 3, 2)).astype(ml_dtypes.float8_e4m3fn).view(np.uint8)
    return words, np.ascontiguousarray(byte.astype(np.uint8).reshape(k // 512, 16, n))


def unpack_weight(words, scales):
    g, p, n, _ = words.shape
    vals = np.ascontiguousarray(words).view(ml_dtypes.float8_e4m3fn).astype(np.float64) * np.repeat(np.exp2(scales.astype(np.float64) - 127.0), 8, axis=1)[..., None]
    return vals.transpose(0, 1, 3, 2).reshape(g * 512, n)


def relu(v):
    return np.maximum(v, 0.0)


K, T, S, D, H, J, V = 512, 2048, 512, 4, 512, 256, 128


def setup_inputs():
    n = np.random.standard_normal
    s = mx_kscale(K)[:, None]
    u = mx_kscale(H)
    packed_xT = pack_weight(n((K, T)) * s)
    return {
        "x_words": packed_xT[0],
        "x_scales": packed_xT[1],
        "w1": (n((K, H)) / np.sqrt(K) / s * u).astype(np.float32),
        "w2": (n((K, H)) / np.sqrt(K) / s / u / np.sqrt(H)).astype(np.float32),
        "eT": (n((K, J)) * s).astype(np.float32),
        "offs": striped(np.random.permutation(T)[:S]),
    }


def reference(x_words, x_scales, w1, w2, eT, offs):
    eTq = mxq(f64(eT), 0, "e4m3")
    g = relu(mxq(f64(w2), 0, "e4m3").T @ eTq)
    xq = unpack_weight(x_words, x_scales)[:, unstriped(offs)]
    h = relu(mxq(f64(w1), 0, "e4m3").T @ xq)
    z = (h.reshape(H, V, D).sum(axis=2)) / 4
    y = mxq(g, 0, "e4m3").T @ mxq(z, 0, "e4m3")
    e = np.exp(y - y.max(axis=1, keepdims=True))
    return e / e.sum(axis=1, keepdims=True)

@@ -1,0 +1,161 @@
+from contextlib import ExitStack
+
+import concourse.mybir as mybir
+
+F32 = mybir.dt.float32
+BF16 = mybir.dt.bfloat16
+I32 = mybir.dt.int32
+U32 = mybir.dt.uint32
+U16 = mybir.dt.uint16
+U8 = mybir.dt.uint8
+FP8X4 = mybir.dt.float8_e4m3fn_x4
+ACT = mybir.ActivationFunctionType
+ALU = mybir.AluOpType
+AXIS_X = mybir.AxisListType.X
+
+K, T, S, D, H, J, V = 512, 2048, 512, 4, 512, 256, 128
+P = 128
+PACK = 4
+FLOPS = 2 * K * H * S + 2 * K * H * J + 2 * H * J * V
+
+W1_ENGINES = "SSSSVVVS"
+W2_ENGINES = "VVSSVVSS"
+E_ENGINES = "SV"
+G_ENGINES = "SS"
+
+
+def tile_picked_zproto_relu_p_kernel(tc, x_words, x_scales, w1, w2, eT, offs, out):
+    nc = tc.nc
+    with ExitStack() as ctx:
+        keep = ctx.enter_context(tc.tile_pool(name="keep", bufs=1))
+        psum = ctx.enter_context(tc.psum_pool(name="psum", bufs=1))
+
+        def sbuf(name, shape, dtype):
+            return keep.tile(shape, dtype, name=name, align_bytes=64)
+
+        def round_to_bf16(engine, dst, src):
+            if engine == "S":
+                nc.scalar.activation(out=dst, in_=src, func=ACT.Copy)
+            else:
+                nc.vector.tensor_copy(out=dst, in_=src)
+
+        def quantize(name, grouped, cols):
+            codes = sbuf(name + "_codes", [P, cols], U32)
+            scales = sbuf(name + "_scales", [P, cols], U8)
+            nc.vector.quantize_mx(out=codes[:].bitcast(FP8X4), scales=scales[:], in_=grouped[:])
+            return codes, scales
+
+        def product(dst, lhs, rhs):
+            nc.tensor.matmul_mx(out=dst, lhsT=lhs[0].bitcast(FP8X4), lhsT_scale=lhs[1],
+                                rhs=rhs[0].bitcast(FP8X4), rhs_scale=rhs[1], start=True, stop=True)
+
+        def load_half(name, src, half, width):
+            raw = sbuf("%s_raw%d" % (name, half), [P, PACK, width], F32)
+            nc.sync.dma_start(out=raw[:], in_=src[:, half * width:(half + 1) * width].rearrange("(p j) c -> p j c", j=PACK))
+            return raw
+
+        offsets = keep.tile([P, S // 16], U16, name="offsets")
+        store_scales = sbuf("store_scales", [P, T], U8)
+        store_words = sbuf("store_words", [P, T], U32)
+        nc.vector.memset(store_scales[:].bitcast(I32), 0)
+        w1_raw = [load_half("w1", w1, 0, H // 2)]
+        for r in range(4):
+            nc.sync.dma_start(out=store_scales[r:P:32, :].bitcast(I32), in_=x_scales[0][r:16:4, :].bitcast(I32))
+        nc.sync.dma_start(offsets[:], offs)
+        nc.sync.dma_start(out=store_words[:].bitcast(I32), in_=x_words[0].rearrange("p n t -> p (n t)").bitcast(I32))
+        w1_raw.append(load_half("w1", w1, 1, H // 2))
+        w2_raw = [load_half("w2", w2, half, H // 2) for half in range(2)]
+        e_raw = [load_half("e", eT, half, J // 2) for half in range(2)]
+
+        def weight_tiles(name):
+            return [sbuf("%s_bf%d" % (name, t), [P, P * PACK], BF16) for t in range(PACK)]
+
+        def round_weights(grouped, raw, half, engines):
+            src = raw[:].rearrange("p j (u t i) -> p t u j i", t=PACK, i=4)
+            for t in range(PACK):
+                dst = grouped[t][:, half * 256:(half + 1) * 256].rearrange("p (u i j) -> p u j i", i=4, j=PACK)
+                round_to_bf16(engines[half * PACK + t], dst, src[:, t])
+
+        picked_scales = sbuf("picked_scales", [P, S], U8)
+        nc.vector.tensor_copy(out=picked_scales[:], in_=store_scales[:].indirect(offsets[:]))
+
+        w1_bf = weight_tiles("w1")
+        round_weights(w1_bf, w1_raw[0], 0, W1_ENGINES)
+        picked_words = []
+        for half in range(2):
+            words = sbuf("picked_words%d" % half, [P, S // 2], U32)
+            nc.vector.tensor_copy(out=words[:], in_=store_words[:].indirect(offsets[:, half * 16:(half + 1) * 16]))
+            picked_words.append(words)
+
+        round_weights(w1_bf, w1_raw[1], 1, W1_ENGINES)
+        w1_q = [quantize("w1_%d" % t, w1_bf[t], P) for t in range(PACK)]
+
+        w2_bf = weight_tiles("w2")
+        round_weights(w2_bf, w2_raw[0], 0, W2_ENGINES)
+
+        pair_sums = [sbuf("pair_sums%d" % half, [P, P, PACK], F32) for half in range(2)]
+        z_bf = sbuf("z_bf", [P, V * PACK], BF16)
+
+        def supports(b):
+            bank = psum.tile([P, PACK, P], F32, name="h_bank%d" % b)
+            words = picked_words[b // 2][:, (b % 2) * P:(b % 2 + 1) * P]
+            scales = picked_scales[:, b * P:(b + 1) * P]
+            for t in range(PACK):
+                product(bank[:, t, :], (w1_q[t][0][:], w1_q[t][1][:]), (words, scales))
+            return bank
+
+        def pair_up(b, bank):
+            by_parity = bank[:].rearrange("p t (c e) -> p e c t", e=2)
+            even = sbuf("even%d" % b, [P, P // 2, PACK], F32)
+            nc.scalar.activation(out=even[:], in_=by_parity[:, 0], func=ACT.Relu)
+            nc.vector.scalar_tensor_tensor(out=pair_sums[b // 2][:, (b % 2) * 64:(b % 2 + 1) * 64, :], in0=by_parity[:, 1],
+                                           scalar=0.0, in1=even[:], op0=ALU.max, op1=ALU.add)
+
+        def prototypes(half):
+            pairs = pair_sums[half][:].rearrange("p (v e) t -> p e v t", e=2)
+            dst = z_bf[:, half * 256:(half + 1) * 256].rearrange("p (v t) -> p v t", t=PACK)
+            nc.vector.tensor_tensor(out=dst, in0=pairs[:, 0], in1=pairs[:, 1], op=ALU.add)
+
+        h_banks = [supports(b) for b in range(4)]
+        round_weights(w2_bf, w2_raw[1], 1, W2_ENGINES)
+        w2_q = [quantize("w2_%d" % t, w2_bf[t], P) for t in range(PACK)]
+        e_q = []
+        for half in range(2):
+            e_bf = sbuf("e_bf%d" % half, [P, P * PACK], BF16)
+            round_to_bf16(E_ENGINES[half], e_bf[:].rearrange("p (u i j) -> p u j i", i=4, j=PACK),
+                          e_raw[half][:].rearrange("p j (u i) -> p u j i", i=4))
+            e_q.append(quantize("e%d" % half, e_bf, P))
+        for b in range(4):
+            pair_up(b, h_banks[b])
+        prototypes(0)
+        prototypes(1)
+
+        g_bf = []
+        for half in range(2):
+            bank = psum.tile([P, PACK, P], F32, name="g_bank%d" % half)
+            for t in range(PACK):
+                product(bank[:, t, :], (w2_q[t][0][:], w2_q[t][1][:]), (e_q[half][0][:], e_q[half][1][:]))
+            rounded = sbuf("g_bf%d" % half, [P, P * PACK], BF16)
+            dst = rounded[:].rearrange("p (q t) -> p q t", t=PACK)
+            src = bank[:].rearrange("p t q -> p q t")
+            if G_ENGINES[half] == "S":
+                nc.scalar.activation(out=dst, in_=src, func=ACT.Relu, scale=1.0 / D)
+            else:
+                nc.vector.tensor_scalar(out=dst, in0=src, scalar1=0.0, scalar2=1.0 / D, op0=ALU.max, op1=ALU.mult)
+            g_bf.append(rounded)
+        z_q = quantize("z", z_bf, V)
+
+        for half in range(2):
+            g_q = quantize("g%d" % half, g_bf[half], P)
+            scores = psum.tile([P, V], F32, name="scores%d" % half)
+            product(scores[:], (g_q[0][:], g_q[1][:]), (z_q[0][:], z_q[1][:]))
+            neg_max = sbuf("neg_max%d" % half, [P, 1], F32)
+            nc.vector.tensor_reduce(out=neg_max[:], in_=scores[:], axis=AXIS_X, op=ALU.max, negate=True)
+            weights = sbuf("weights%d" % half, [P, V], F32)
+            total = sbuf("total%d" % half, [P, 1], F32)
+            nc.scalar.activation(out=weights[:], in_=scores[:], func=ACT.Exp, bias=neg_max[:], accum_out=total[:])
+            inverse = sbuf("inverse%d" % half, [P, 1], F32)
+            nc.vector.reciprocal(out=inverse[:], in_=total[:])
+            result = sbuf("result%d" % half, [P, V], F32)
+            nc.vector.tensor_scalar(out=result[:], in0=weights[:], scalar1=inverse[:], scalar2=None, op0=ALU.mult)
+            nc.sync.dma_start(out=out[half * P:(half + 1) * P, :], in_=result[:])

@@ -18,11 +18,6 @@ P = 128
 PACK = 4
 FLOPS = 2 * K * H * S + 2 * K * H * J + 2 * H * J * V
 
-W1_ENGINES = "SSSSVVVS"
-W2_ENGINES = "VVSSVVSS"
-E_ENGINES = "SV"
-G_ENGINES = "SS"
-
 
 def tile_picked_zproto_relu_p_kernel(tc, x_words, x_scales, w1, w2, eT, offs, out):
     nc = tc.nc
@@ -30,20 +25,25 @@ def tile_picked_zproto_relu_p_kernel(tc, x_words, x_scales, w1, w2, eT, offs, ou
         keep = ctx.enter_context(tc.tile_pool(name="keep", bufs=1))
         psum = ctx.enter_context(tc.psum_pool(name="psum", bufs=1))
 
-        def sbuf(name, shape, dtype):
-            return keep.tile(shape, dtype, name=name, align_bytes=64)
+        def sbuf(name, shape, dtype, tag=None):
+            return keep.tile(shape, dtype, name=name, tag=tag or name, align_bytes=64)
 
         def round_to_bf16(engine, dst, src):
             if engine == "S":
                 nc.scalar.activation(out=dst, in_=src, func=ACT.Copy)
-            else:
+            elif engine == "V":
                 nc.vector.tensor_copy(out=dst, in_=src)
+            else:
+                nc.gpsimd.tensor_scalar(out=dst, in0=src, scalar1=1.0, scalar2=0.0, op0=ALU.mult, op1=ALU.add)
 
-        def quantize(name, grouped, cols):
-            codes = sbuf(name + "_codes", [P, cols], U32)
-            scales = sbuf(name + "_scales", [P, cols], U8)
-            nc.vector.quantize_mx(out=codes[:].bitcast(FP8X4), scales=scales[:], in_=grouped[:])
-            return codes, scales
+        def mx_tiles(name, cols):
+            return sbuf(name + "_codes", [P, cols], U32), sbuf(name + "_scales", [P, cols], U8)
+
+        def quantize(dst, src):
+            nc.vector.quantize_mx(out=dst[0][:].bitcast(FP8X4), scales=dst[1][:], in_=src)
+
+        def columns(operand, start, stop):
+            return operand[0][:, start:stop], operand[1][:, start:stop]
 
         def product(dst, lhs, rhs):
             nc.tensor.matmul_mx(out=dst, lhsT=lhs[0].bitcast(FP8X4), lhsT_scale=lhs[1],
@@ -57,105 +57,156 @@ def tile_picked_zproto_relu_p_kernel(tc, x_words, x_scales, w1, w2, eT, offs, ou
         offsets = keep.tile([P, S // 16], U16, name="offsets")
         store_scales = sbuf("store_scales", [P, T], U8)
         store_words = sbuf("store_words", [P, T], U32)
-        nc.vector.memset(store_scales[:].bitcast(I32), 0)
-        w1_raw = [load_half("w1", w1, 0, H // 2)]
-        for r in range(4):
-            nc.sync.dma_start(out=store_scales[r:P:32, :].bitcast(I32), in_=x_scales[0][r:16:4, :].bitcast(I32))
-        nc.sync.dma_start(offsets[:], offs)
-        nc.sync.dma_start(out=store_words[:].bitcast(I32), in_=x_words[0].rearrange("p n t -> p (n t)").bitcast(I32))
-        w1_raw.append(load_half("w1", w1, 1, H // 2))
-        w2_raw = [load_half("w2", w2, half, H // 2) for half in range(2)]
-        e_raw = [load_half("e", eT, half, J // 2) for half in range(2)]
-
-        def weight_tiles(name):
-            return [sbuf("%s_bf%d" % (name, t), [P, P * PACK], BF16) for t in range(PACK)]
-
-        def round_weights(grouped, raw, half, engines):
-            src = raw[:].rearrange("p j (u t i) -> p t u j i", t=PACK, i=4)
-            for t in range(PACK):
-                dst = grouped[t][:, half * 256:(half + 1) * 256].rearrange("p (u i j) -> p u j i", i=4, j=PACK)
-                round_to_bf16(engines[half * PACK + t], dst, src[:, t])
-
         picked_scales = sbuf("picked_scales", [P, S], U8)
-        nc.vector.tensor_copy(out=picked_scales[:], in_=store_scales[:].indirect(offsets[:]))
-
-        w1_bf = weight_tiles("w1")
-        round_weights(w1_bf, w1_raw[0], 0, W1_ENGINES)
-        picked_words = []
-        for half in range(2):
-            words = sbuf("picked_words%d" % half, [P, S // 2], U32)
-            nc.vector.tensor_copy(out=words[:], in_=store_words[:].indirect(offsets[:, half * 16:(half + 1) * 16]))
-            picked_words.append(words)
-
-        round_weights(w1_bf, w1_raw[1], 1, W1_ENGINES)
-        w1_q = [quantize("w1_%d" % t, w1_bf[t], P) for t in range(PACK)]
-
-        w2_bf = weight_tiles("w2")
-        round_weights(w2_bf, w2_raw[0], 0, W2_ENGINES)
-
-        pair_sums = [sbuf("pair_sums%d" % half, [P, P, PACK], F32) for half in range(2)]
+        picked_words = [sbuf("picked_words%d" % half, [P, S // 2], U32) for half in range(2)]
+        w1_bf = sbuf("w1_bf", [P, H * PACK], BF16)
+        w2_bf = sbuf("w2_bf", [P, H * PACK], BF16)
+        w1_q = mx_tiles("w1", H)
+        w2_q = mx_tiles("w2", H)
+        e_bf = [sbuf("e_bf%d" % half, [P, P * PACK], BF16) for half in range(2)]
+        g_bf = [sbuf("g_bf%d" % half, [P, P * PACK], BF16) for half in range(2)]
+        e_q = [mx_tiles("e%d" % half, P) for half in range(2)]
+        g_q = [mx_tiles("g%d" % half, P) for half in range(2)]
+        z_q = mx_tiles("z", V)
         z_bf = sbuf("z_bf", [P, V * PACK], BF16)
+        pair_sums = sbuf("pair_sums", [P, 2 * V * PACK], F32)
+        h_banks = [psum.tile([P, PACK, P], F32, name="h_bank%d" % b) for b in range(4)]
+        g_banks = [psum.tile([P, PACK, P], F32, name="g_bank%d" % b) for b in range(2)]
+        scores = [psum.tile([P, V], F32, name="scores%d" % b) for b in range(2)]
+        running = {}
+
+        def gather_scales():
+            nc.vector.tensor_copy(out=picked_scales[:], in_=store_scales[:].indirect(offsets[:]))
+
+        def gather_words(half):
+            nc.vector.tensor_copy(out=picked_words[half][:], in_=store_words[:].indirect(offsets[:, half * 16:(half + 1) * 16]))
+
+        def round_weights(grouped, raw, half, first, last, engine):
+            src = raw[:].rearrange("p j (u t i) -> p t u j i", t=PACK, i=4)
+            dst = grouped[:].rearrange("p (t h u i j) -> p h t u j i", t=PACK, h=2, i=4, j=PACK)[:, half]
+            if engine == "V" or False:
+                round_to_bf16(engine, dst[:, first:last + 1], src[:, first:last + 1])
+            else:
+                for t in range(first, last + 1):
+                    round_to_bf16(engine, dst[:, t], src[:, t])
+
+        def quantize_slots(dst, grouped, first, last):
+            quantize(columns(dst, first * P, (last + 1) * P), grouped[:, first * P * PACK:(last + 1) * P * PACK])
+
+        def warm(n):
+            product(scores[1][:, 0:n], (picked_words[0][:, 0:P], picked_scales[:, 0:P]), (picked_words[0][:, 0:n], picked_scales[:, 0:n]))
 
         def supports(b):
-            bank = psum.tile([P, PACK, P], F32, name="h_bank%d" % b)
             words = picked_words[b // 2][:, (b % 2) * P:(b % 2 + 1) * P]
             scales = picked_scales[:, b * P:(b + 1) * P]
             for t in range(PACK):
-                product(bank[:, t, :], (w1_q[t][0][:], w1_q[t][1][:]), (words, scales))
-            return bank
+                product(h_banks[b][:, t, :], columns(w1_q, t * P, (t + 1) * P), (words, scales))
 
-        def pair_up(b, bank):
-            by_parity = bank[:].rearrange("p t (c e) -> p e c t", e=2)
-            even = sbuf("even%d" % b, [P, P // 2, PACK], F32)
-            nc.scalar.activation(out=even[:], in_=by_parity[:, 0], func=ACT.Relu)
-            nc.vector.scalar_tensor_tensor(out=pair_sums[b // 2][:, (b % 2) * 64:(b % 2 + 1) * 64, :], in0=by_parity[:, 1],
-                                           scalar=0.0, in1=even[:], op0=ALU.max, op1=ALU.add)
+        def pair_up(b):
+            by_parity = h_banks[b][:].rearrange("p t (c e) -> p e c t", e=2)
+            if "even" not in running:
+                running["even"] = sbuf("even", [P, 1024], F32, tag="e_raw0")
+            even = running["even"][:, b * 256:(b + 1) * 256].rearrange("p (c t) -> p c t", t=PACK)
+            nc.scalar.activation(out=even, in_=by_parity[:, 0], func=ACT.Relu)
+            dst = pair_sums[:, b * 256:(b + 1) * 256].rearrange("p (c t) -> p c t", t=PACK)
+            nc.vector.scalar_tensor_tensor(out=dst, in0=by_parity[:, 1], scalar=0.0, in1=even, op0=ALU.max, op1=ALU.add)
 
-        def prototypes(half):
-            pairs = pair_sums[half][:].rearrange("p (v e) t -> p e v t", e=2)
-            dst = z_bf[:, half * 256:(half + 1) * 256].rearrange("p (v t) -> p v t", t=PACK)
-            nc.vector.tensor_tensor(out=dst, in0=pairs[:, 0], in1=pairs[:, 1], op=ALU.add)
+        def add_member(b, d):
+            member = h_banks[b][:].rearrange("p t (v d) -> p d v t", d=D)[:, d]
+            if d == D - 1:
+                dst = z_bf[:, b * P:(b + 1) * P].rearrange("p (v t) -> p v t", t=PACK)
+            else:
+                tile = sbuf("sum%d_%d" % (b, d), [P, P // D, PACK], F32)
+                dst = tile[:]
+            if d == 0:
+                nc.scalar.activation(out=dst, in_=member, func=ACT.Relu)
+            else:
+                nc.vector.scalar_tensor_tensor(out=dst, in0=member, scalar=0.0, in1=running[b], op0=ALU.max, op1=ALU.add)
+            running[b] = dst
 
-        h_banks = [supports(b) for b in range(4)]
-        round_weights(w2_bf, w2_raw[1], 1, W2_ENGINES)
-        w2_q = [quantize("w2_%d" % t, w2_bf[t], P) for t in range(PACK)]
-        e_q = []
-        for half in range(2):
-            e_bf = sbuf("e_bf%d" % half, [P, P * PACK], BF16)
-            round_to_bf16(E_ENGINES[half], e_bf[:].rearrange("p (u i j) -> p u j i", i=4, j=PACK),
-                          e_raw[half][:].rearrange("p j (u i) -> p u j i", i=4))
-            e_q.append(quantize("e%d" % half, e_bf, P))
-        for b in range(4):
-            pair_up(b, h_banks[b])
-        prototypes(0)
-        prototypes(1)
+        def prototypes(first, stop):
+            pairs = pair_sums[:].rearrange("p (v e t) -> p e v t", e=2, t=PACK)
+            dst = z_bf[:].rearrange("p (v t) -> p v t", t=PACK)
+            nc.vector.tensor_tensor(out=dst[:, first:stop], in0=pairs[:, 0, first:stop], in1=pairs[:, 1, first:stop], op=ALU.add)
 
-        g_bf = []
-        for half in range(2):
-            bank = psum.tile([P, PACK, P], F32, name="g_bank%d" % half)
+        def round_queries(half, raw, first, stop, engine):
+            dst = e_bf[half][:, first * PACK:stop * PACK].rearrange("p (u i j) -> p u j i", i=4, j=PACK)
+            round_to_bf16(engine, dst, raw[:, :, first:stop].rearrange("p j (u i) -> p u j i", i=4))
+
+        def queries(half):
             for t in range(PACK):
-                product(bank[:, t, :], (w2_q[t][0][:], w2_q[t][1][:]), (e_q[half][0][:], e_q[half][1][:]))
-            rounded = sbuf("g_bf%d" % half, [P, P * PACK], BF16)
-            dst = rounded[:].rearrange("p (q t) -> p q t", t=PACK)
-            src = bank[:].rearrange("p t q -> p q t")
-            if G_ENGINES[half] == "S":
+                product(g_banks[half][:, t, :], columns(w2_q, t * P, (t + 1) * P), columns(e_q[half], 0, P))
+
+        def round_features(half, engine):
+            dst = g_bf[half][:].rearrange("p (q t) -> p q t", t=PACK)
+            src = g_banks[half][:].rearrange("p t q -> p q t")
+            if engine == "S":
                 nc.scalar.activation(out=dst, in_=src, func=ACT.Relu, scale=1.0 / D)
             else:
                 nc.vector.tensor_scalar(out=dst, in0=src, scalar1=0.0, scalar2=1.0 / D, op0=ALU.max, op1=ALU.mult)
-            g_bf.append(rounded)
-        z_q = quantize("z", z_bf, V)
 
-        for half in range(2):
-            g_q = quantize("g%d" % half, g_bf[half], P)
-            scores = psum.tile([P, V], F32, name="scores%d" % half)
-            product(scores[:], (g_q[0][:], g_q[1][:]), (z_q[0][:], z_q[1][:]))
+        def score(half):
+            product(scores[half][:, 0:V], columns(g_q[half], 0, P), columns(z_q, 0, V))
+
+        def softmax(half):
             neg_max = sbuf("neg_max%d" % half, [P, 1], F32)
-            nc.vector.tensor_reduce(out=neg_max[:], in_=scores[:], axis=AXIS_X, op=ALU.max, negate=True)
+            nc.vector.tensor_reduce(out=neg_max[:], in_=scores[half][:, 0:V], axis=AXIS_X, op=ALU.max, negate=True)
             weights = sbuf("weights%d" % half, [P, V], F32)
             total = sbuf("total%d" % half, [P, 1], F32)
-            nc.scalar.activation(out=weights[:], in_=scores[:], func=ACT.Exp, bias=neg_max[:], accum_out=total[:])
+            nc.scalar.activation(out=weights[:], in_=scores[half][:, 0:V], func=ACT.Exp, bias=neg_max[:], accum_out=total[:])
             inverse = sbuf("inverse%d" % half, [P, 1], F32)
             nc.vector.reciprocal(out=inverse[:], in_=total[:])
             result = sbuf("result%d" % half, [P, V], F32)
             nc.vector.tensor_scalar(out=result[:], in0=weights[:], scalar1=inverse[:], scalar2=None, op0=ALU.mult)
             nc.sync.dma_start(out=out[half * P:(half + 1) * P, :], in_=result[:])
+
+        nc.vector.memset(store_scales[:].bitcast(I32), 0)
+        w1_raw0 = load_half("w1", w1, 0, H // 2)
+        for r in range(4):
+            nc.sync.dma_start(out=store_scales[r:P:32, :].bitcast(I32), in_=x_scales[0][r:16:4, :].bitcast(I32))
+        nc.sync.dma_start(offsets[:], offs)
+        nc.sync.dma_start(out=store_words[:].bitcast(I32), in_=x_words[0].rearrange("p n t -> p (n t)").bitcast(I32))
+        w1_raw1 = load_half("w1", w1, 1, H // 2)
+        w2_raw0 = load_half("w2", w2, 0, H // 2)
+        w2_raw1 = load_half("w2", w2, 1, H // 2)
+        e_raw0 = load_half("e", eT, 0, J // 2)
+        e_raw1 = load_half("e", eT, 1, J // 2)
+        round_weights(w1_bf, w1_raw0, 0, 0, 3, "S")
+        gather_scales()
+        gather_words(0)
+        gather_words(1)
+        round_weights(w1_bf, w1_raw1, 1, 0, 2, "V")
+        round_weights(w1_bf, w1_raw1, 1, 3, 3, "S")
+        quantize_slots(w1_q, w1_bf, 0, 1)
+        quantize_slots(w1_q, w1_bf, 2, 3)
+        supports(0)
+        supports(1)
+        supports(2)
+        supports(3)
+        round_weights(w2_bf, w2_raw0, 0, 0, 1, "V")
+        round_weights(w2_bf, w2_raw0, 0, 2, 3, "S")
+        round_weights(w2_bf, w2_raw1, 1, 0, 1, "V")
+        round_weights(w2_bf, w2_raw1, 1, 2, 3, "S")
+        quantize_slots(w2_q, w2_bf, 0, 1)
+        round_queries(0, e_raw0, 0, 128, "S")
+        quantize_slots(w2_q, w2_bf, 2, 3)
+        round_queries(1, e_raw1, 0, 128, "V")
+        quantize(e_q[0], e_bf[0][:])
+        quantize(e_q[1], e_bf[1][:])
+        queries(0)
+        queries(1)
+        pair_up(0)
+        pair_up(1)
+        pair_up(2)
+        pair_up(3)
+        prototypes(0 * 64, 0 * 64 + 64)
+        prototypes(1 * 64, 1 * 64 + 64)
+        round_features(0, "S")
+        round_features(1, "S")
+        quantize(g_q[0], g_bf[0][:])
+        quantize(z_q, z_bf[:])
+        quantize(g_q[1], g_bf[1][:])
+        score(0)
+        score(1)
+        softmax(0)
+        softmax(1)

@@ -69,7 +69,6 @@ def tile_picked_zproto_relu_p_kernel(tc, x_words, x_scales, w1, w2, eT, offs, ou
         g_q = [mx_tiles("g%d" % half, P) for half in range(2)]
         z_q = mx_tiles("z", V)
         z_bf = sbuf("z_bf", [P, V * PACK], BF16)
-        pair_sums = sbuf("pair_sums", [P, 2 * V * PACK], F32)
         h_banks = [psum.tile([P, PACK, P], F32, name="h_bank%d" % b) for b in range(4)]
         g_banks = [psum.tile([P, PACK, P], F32, name="g_bank%d" % b) for b in range(2)]
         scores = [psum.tile([P, V], F32, name="scores%d" % b) for b in range(2)]
@@ -93,6 +92,10 @@ def tile_picked_zproto_relu_p_kernel(tc, x_words, x_scales, w1, w2, eT, offs, ou
         def quantize_slots(dst, grouped, first, last):
             quantize(columns(dst, first * P, (last + 1) * P), grouped[:, first * P * PACK:(last + 1) * P * PACK])
 
+        def quantize_half(dst, grouped, half, t):
+            first = t * P + half * 64
+            quantize(columns(dst, first, first + 64), grouped[:, first * PACK:(first + 64) * PACK])
+
         def warm(n):
             product(scores[1][:, 0:n], (picked_words[0][:, 0:P], picked_scales[:, 0:P]), (picked_words[0][:, 0:n], picked_scales[:, 0:n]))
 
@@ -102,12 +105,16 @@ def tile_picked_zproto_relu_p_kernel(tc, x_words, x_scales, w1, w2, eT, offs, ou
             for t in range(PACK):
                 product(h_banks[b][:, t, :], columns(w1_q, t * P, (t + 1) * P), (words, scales))
 
-        def pair_up(b):
+        def pair_up(b, held=True):
             by_parity = h_banks[b][:].rearrange("p t (c e) -> p e c t", e=2)
-            if "even" not in running:
+            if held and "even" not in running:
                 running["even"] = sbuf("even", [P, 1024], F32, tag="e_raw0")
-            even = running["even"][:, b * 256:(b + 1) * 256].rearrange("p (c t) -> p c t", t=PACK)
+            home = running["even"] if held else sbuf("even%d" % b, [P, 1024], F32, tag="w2_raw0")
+            even = home[:, b * 256:(b + 1) * 256].rearrange("p (c t) -> p c t", t=PACK)
             nc.scalar.activation(out=even, in_=by_parity[:, 0], func=ACT.Relu)
+            if "pairs" not in running:
+                running["pairs"] = sbuf("pair_sums", [P, 2 * V * PACK], F32, tag="w2_raw1")
+            pair_sums = running["pairs"]
             dst = pair_sums[:, b * 256:(b + 1) * 256].rearrange("p (c t) -> p c t", t=PACK)
             nc.vector.scalar_tensor_tensor(out=dst, in0=by_parity[:, 1], scalar=0.0, in1=even, op0=ALU.max, op1=ALU.add)
 
@@ -125,7 +132,7 @@ def tile_picked_zproto_relu_p_kernel(tc, x_words, x_scales, w1, w2, eT, offs, ou
             running[b] = dst
 
         def prototypes(first, stop):
-            pairs = pair_sums[:].rearrange("p (v e t) -> p e v t", e=2, t=PACK)
+            pairs = running["pairs"][:].rearrange("p (v e t) -> p e v t", e=2, t=PACK)
             dst = z_bf[:].rearrange("p (v t) -> p v t", t=PACK)
             nc.vector.tensor_tensor(out=dst[:, first:stop], in0=pairs[:, 0, first:stop], in1=pairs[:, 1, first:stop], op=ALU.add)
 
@@ -162,40 +169,46 @@ def tile_picked_zproto_relu_p_kernel(tc, x_words, x_scales, w1, w2, eT, offs, ou
 
         nc.vector.memset(store_scales[:].bitcast(I32), 0)
         w1_raw0 = load_half("w1", w1, 0, H // 2)
+        nc.sync.dma_start(offsets[:], offs)
+        w1_raw1 = load_half("w1", w1, 1, H // 2)
         for r in range(4):
             nc.sync.dma_start(out=store_scales[r:P:32, :].bitcast(I32), in_=x_scales[0][r:16:4, :].bitcast(I32))
-        nc.sync.dma_start(offsets[:], offs)
         nc.sync.dma_start(out=store_words[:].bitcast(I32), in_=x_words[0].rearrange("p n t -> p (n t)").bitcast(I32))
-        w1_raw1 = load_half("w1", w1, 1, H // 2)
         w2_raw0 = load_half("w2", w2, 0, H // 2)
         w2_raw1 = load_half("w2", w2, 1, H // 2)
         e_raw0 = load_half("e", eT, 0, J // 2)
         e_raw1 = load_half("e", eT, 1, J // 2)
         round_weights(w1_bf, w1_raw0, 0, 0, 3, "S")
+        round_weights(w1_bf, w1_raw1, 1, 0, 1, "V")
+        round_weights(w1_bf, w1_raw1, 1, 2, 3, "S")
         gather_scales()
-        gather_words(0)
-        gather_words(1)
-        round_weights(w1_bf, w1_raw1, 1, 0, 2, "V")
-        round_weights(w1_bf, w1_raw1, 1, 3, 3, "S")
         quantize_slots(w1_q, w1_bf, 0, 1)
         quantize_slots(w1_q, w1_bf, 2, 3)
+        gather_words(0)
+        gather_words(1)
         supports(0)
         supports(1)
         supports(2)
         supports(3)
         round_weights(w2_bf, w2_raw0, 0, 0, 1, "V")
         round_weights(w2_bf, w2_raw0, 0, 2, 3, "S")
+        quantize_half(w2_q, w2_bf, 0, 0)
+        quantize_half(w2_q, w2_bf, 0, 1)
+        quantize_half(w2_q, w2_bf, 0, 2)
+        quantize_half(w2_q, w2_bf, 0, 3)
         round_weights(w2_bf, w2_raw1, 1, 0, 1, "V")
         round_weights(w2_bf, w2_raw1, 1, 2, 3, "S")
-        quantize_slots(w2_q, w2_bf, 0, 1)
+        quantize_half(w2_q, w2_bf, 1, 2)
+        quantize_half(w2_q, w2_bf, 1, 0)
+        quantize_half(w2_q, w2_bf, 1, 1)
+        quantize_half(w2_q, w2_bf, 1, 3)
         round_queries(0, e_raw0, 0, 128, "S")
-        quantize_slots(w2_q, w2_bf, 2, 3)
         round_queries(1, e_raw1, 0, 128, "V")
         quantize(e_q[0], e_bf[0][:])
         quantize(e_q[1], e_bf[1][:])
         queries(0)
         queries(1)
-        pair_up(0)
+        pair_up(0, False)
         pair_up(1)
         pair_up(2)
         pair_up(3)

from contextlib import ExitStack

import concourse.mybir as mybir

F32 = mybir.dt.float32
BF16 = mybir.dt.bfloat16
I32 = mybir.dt.int32
U32 = mybir.dt.uint32
U16 = mybir.dt.uint16
U8 = mybir.dt.uint8
FP8X4 = mybir.dt.float8_e4m3fn_x4
ACT = mybir.ActivationFunctionType
ALU = mybir.AluOpType
AXIS_X = mybir.AxisListType.X

K, T, S, D, H, J, V = 512, 2048, 512, 4, 512, 256, 128
P = 128
PACK = 4
FLOPS = 2 * K * H * S + 2 * K * H * J + 2 * H * J * V


def tile_picked_zproto_relu_p_kernel(tc, x_words, x_scales, w1, w2, eT, offs, out):
    nc = tc.nc
    with ExitStack() as ctx:
        keep = ctx.enter_context(tc.tile_pool(name="keep", bufs=1))
        psum = ctx.enter_context(tc.psum_pool(name="psum", bufs=1))

        def sbuf(name, shape, dtype, tag=None):
            return keep.tile(shape, dtype, name=name, tag=tag or name, align_bytes=64)

        def round_to_bf16(engine, dst, src):
            if engine == "S":
                nc.scalar.activation(out=dst, in_=src, func=ACT.Copy)
            elif engine == "V":
                nc.vector.tensor_copy(out=dst, in_=src)
            else:
                nc.gpsimd.tensor_scalar(out=dst, in0=src, scalar1=1.0, scalar2=0.0, op0=ALU.mult, op1=ALU.add)

        def mx_tiles(name, cols):
            return sbuf(name + "_codes", [P, cols], U32), sbuf(name + "_scales", [P, cols], U8)

        def quantize(dst, src):
            nc.vector.quantize_mx(out=dst[0][:].bitcast(FP8X4), scales=dst[1][:], in_=src)

        def columns(operand, start, stop):
            return operand[0][:, start:stop], operand[1][:, start:stop]

        def product(dst, lhs, rhs):
            nc.tensor.matmul_mx(out=dst, lhsT=lhs[0].bitcast(FP8X4), lhsT_scale=lhs[1],
                                rhs=rhs[0].bitcast(FP8X4), rhs_scale=rhs[1], start=True, stop=True)

        def load_half(name, src, half, width):
            raw = sbuf("%s_raw%d" % (name, half), [P, PACK, width], F32)
            nc.sync.dma_start(out=raw[:], in_=src[:, half * width:(half + 1) * width].rearrange("(p j) c -> p j c", j=PACK))
            return raw

        offsets = keep.tile([P, S // 16], U16, name="offsets")
        store_scales = sbuf("store_scales", [P, T], U8)
        store_words = sbuf("store_words", [P, T], U32)
        picked_scales = sbuf("picked_scales", [P, S], U8)
        picked_words = [sbuf("picked_words%d" % half, [P, S // 2], U32) for half in range(2)]
        w1_bf = sbuf("w1_bf", [P, H * PACK], BF16)
        w2_bf = sbuf("w2_bf", [P, H * PACK], BF16)
        w1_q = mx_tiles("w1", H)
        w2_q = mx_tiles("w2", H)
        e_bf = [sbuf("e_bf%d" % half, [P, P * PACK], BF16) for half in range(2)]
        g_bf = [sbuf("g_bf%d" % half, [P, P * PACK], BF16) for half in range(2)]
        e_q = [mx_tiles("e%d" % half, P) for half in range(2)]
        g_q = [mx_tiles("g%d" % half, P) for half in range(2)]
        z_q = mx_tiles("z", V)
        z_bf = sbuf("z_bf", [P, V * PACK], BF16)
        h_banks = [psum.tile([P, PACK, P], F32, name="h_bank%d" % b) for b in range(4)]
        g_banks = [psum.tile([P, PACK, P], F32, name="g_bank%d" % b) for b in range(2)]
        scores = [psum.tile([P, V], F32, name="scores%d" % b) for b in range(2)]
        running = {}

        def gather_scales():
            nc.vector.tensor_copy(out=picked_scales[:], in_=store_scales[:].indirect(offsets[:]))

        def gather_words(half):
            nc.vector.tensor_copy(out=picked_words[half][:], in_=store_words[:].indirect(offsets[:, half * 16:(half + 1) * 16]))

        def round_weights(grouped, raw, half, first, last, engine):
            src = raw[:].rearrange("p j (u t i) -> p t u j i", t=PACK, i=4)
            dst = grouped[:].rearrange("p (t h u i j) -> p h t u j i", t=PACK, h=2, i=4, j=PACK)[:, half]
            if engine == "V" or False:
                round_to_bf16(engine, dst[:, first:last + 1], src[:, first:last + 1])
            else:
                for t in range(first, last + 1):
                    round_to_bf16(engine, dst[:, t], src[:, t])

        def quantize_slots(dst, grouped, first, last):
            quantize(columns(dst, first * P, (last + 1) * P), grouped[:, first * P * PACK:(last + 1) * P * PACK])

        def quantize_half(dst, grouped, half, t):
            first = t * P + half * 64
            quantize(columns(dst, first, first + 64), grouped[:, first * PACK:(first + 64) * PACK])

        def warm(n):
            product(scores[1][:, 0:n], (picked_words[0][:, 0:P], picked_scales[:, 0:P]), (picked_words[0][:, 0:n], picked_scales[:, 0:n]))

        def supports(b):
            words = picked_words[b // 2][:, (b % 2) * P:(b % 2 + 1) * P]
            scales = picked_scales[:, b * P:(b + 1) * P]
            for t in range(PACK):
                product(h_banks[b][:, t, :], columns(w1_q, t * P, (t + 1) * P), (words, scales))

        def pair_up(b, held=True):
            by_parity = h_banks[b][:].rearrange("p t (c e) -> p e c t", e=2)
            if held and "even" not in running:
                running["even"] = sbuf("even", [P, 1024], F32, tag="e_raw0")
            home = running["even"] if held else sbuf("even%d" % b, [P, 1024], F32, tag="w2_raw0")
            even = home[:, b * 256:(b + 1) * 256].rearrange("p (c t) -> p c t", t=PACK)
            nc.scalar.activation(out=even, in_=by_parity[:, 0], func=ACT.Relu)
            if "pairs" not in running:
                running["pairs"] = sbuf("pair_sums", [P, 2 * V * PACK], F32, tag="w2_raw1")
            pair_sums = running["pairs"]
            dst = pair_sums[:, b * 256:(b + 1) * 256].rearrange("p (c t) -> p c t", t=PACK)
            nc.vector.scalar_tensor_tensor(out=dst, in0=by_parity[:, 1], scalar=0.0, in1=even, op0=ALU.max, op1=ALU.add)

        def add_member(b, d):
            member = h_banks[b][:].rearrange("p t (v d) -> p d v t", d=D)[:, d]
            if d == D - 1:
                dst = z_bf[:, b * P:(b + 1) * P].rearrange("p (v t) -> p v t", t=PACK)
            else:
                tile = sbuf("sum%d_%d" % (b, d), [P, P // D, PACK], F32)
                dst = tile[:]
            if d == 0:
                nc.scalar.activation(out=dst, in_=member, func=ACT.Relu)
            else:
                nc.vector.scalar_tensor_tensor(out=dst, in0=member, scalar=0.0, in1=running[b], op0=ALU.max, op1=ALU.add)
            running[b] = dst

        def prototypes(first, stop):
            pairs = running["pairs"][:].rearrange("p (v e t) -> p e v t", e=2, t=PACK)
            dst = z_bf[:].rearrange("p (v t) -> p v t", t=PACK)
            nc.vector.tensor_tensor(out=dst[:, first:stop], in0=pairs[:, 0, first:stop], in1=pairs[:, 1, first:stop], op=ALU.add)

        def round_queries(half, raw, first, stop, engine):
            dst = e_bf[half][:, first * PACK:stop * PACK].rearrange("p (u i j) -> p u j i", i=4, j=PACK)
            round_to_bf16(engine, dst, raw[:, :, first:stop].rearrange("p j (u i) -> p u j i", i=4))

        def queries(half):
            for t in range(PACK):
                product(g_banks[half][:, t, :], columns(w2_q, t * P, (t + 1) * P), columns(e_q[half], 0, P))

        def round_features(half, engine):
            dst = g_bf[half][:].rearrange("p (q t) -> p q t", t=PACK)
            src = g_banks[half][:].rearrange("p t q -> p q t")
            if engine == "S":
                nc.scalar.activation(out=dst, in_=src, func=ACT.Relu, scale=1.0 / D)
            else:
                nc.vector.tensor_scalar(out=dst, in0=src, scalar1=0.0, scalar2=1.0 / D, op0=ALU.max, op1=ALU.mult)

        def score(half):
            product(scores[half][:, 0:V], columns(g_q[half], 0, P), columns(z_q, 0, V))

        def softmax(half):
            neg_max = sbuf("neg_max%d" % half, [P, 1], F32)
            nc.vector.tensor_reduce(out=neg_max[:], in_=scores[half][:, 0:V], axis=AXIS_X, op=ALU.max, negate=True)
            weights = sbuf("weights%d" % half, [P, V], F32)
            total = sbuf("total%d" % half, [P, 1], F32)
            nc.scalar.activation(out=weights[:], in_=scores[half][:, 0:V], func=ACT.Exp, bias=neg_max[:], accum_out=total[:])
            inverse = sbuf("inverse%d" % half, [P, 1], F32)
            nc.vector.reciprocal(out=inverse[:], in_=total[:])
            result = sbuf("result%d" % half, [P, V], F32)
            nc.vector.tensor_scalar(out=result[:], in0=weights[:], scalar1=inverse[:], scalar2=None, op0=ALU.mult)
            nc.sync.dma_start(out=out[half * P:(half + 1) * P, :], in_=result[:])

        nc.vector.memset(store_scales[:].bitcast(I32), 0)
        w1_raw0 = load_half("w1", w1, 0, H // 2)
        nc.sync.dma_start(offsets[:], offs)
        w1_raw1 = load_half("w1", w1, 1, H // 2)
        for r in range(4):
            nc.sync.dma_start(out=store_scales[r:P:32, :].bitcast(I32), in_=x_scales[0][r:16:4, :].bitcast(I32))
        nc.sync.dma_start(out=store_words[:].bitcast(I32), in_=x_words[0].rearrange("p n t -> p (n t)").bitcast(I32))
        w2_raw0 = load_half("w2", w2, 0, H // 2)
        w2_raw1 = load_half("w2", w2, 1, H // 2)
        e_raw0 = load_half("e", eT, 0, J // 2)
        e_raw1 = load_half("e", eT, 1, J // 2)
        round_weights(w1_bf, w1_raw0, 0, 0, 3, "S")
        round_weights(w1_bf, w1_raw1, 1, 0, 1, "V")
        round_weights(w1_bf, w1_raw1, 1, 2, 3, "S")
        gather_scales()
        quantize_slots(w1_q, w1_bf, 0, 1)
        quantize_slots(w1_q, w1_bf, 2, 3)
        gather_words(0)
        gather_words(1)
        supports(0)
        supports(1)
        supports(2)
        supports(3)
        round_weights(w2_bf, w2_raw0, 0, 0, 1, "V")
        round_weights(w2_bf, w2_raw0, 0, 2, 3, "S")
        quantize_half(w2_q, w2_bf, 0, 0)
        quantize_half(w2_q, w2_bf, 0, 1)
        quantize_half(w2_q, w2_bf, 0, 2)
        quantize_half(w2_q, w2_bf, 0, 3)
        round_weights(w2_bf, w2_raw1, 1, 0, 1, "V")
        round_weights(w2_bf, w2_raw1, 1, 2, 3, "S")
        quantize_half(w2_q, w2_bf, 1, 2)
        quantize_half(w2_q, w2_bf, 1, 0)
        quantize_half(w2_q, w2_bf, 1, 1)
        quantize_half(w2_q, w2_bf, 1, 3)
        round_queries(0, e_raw0, 0, 128, "S")
        round_queries(1, e_raw1, 0, 128, "V")
        quantize(e_q[0], e_bf[0][:])
        quantize(e_q[1], e_bf[1][:])
        queries(0)
        queries(1)
        pair_up(0, False)
        pair_up(1)
        pair_up(2)
        pair_up(3)
        prototypes(0 * 64, 0 * 64 + 64)
        prototypes(1 * 64, 1 * 64 + 64)
        round_features(0, "S")
        round_features(1, "S")
        quantize(g_q[0], g_bf[0][:])
        quantize(z_q, z_bf[:])
        quantize(g_q[1], g_bf[1][:])
        score(0)
        score(1)
        softmax(0)
        softmax(1)
